import numpy as np
import ml_dtypes


def mxq(x, axis, fmt="e4m3"):
    dtype, down = {"e4m3": (ml_dtypes.float8_e4m3fn, 7), "e5m2": (ml_dtypes.float8_e5m2, 14)}[fmt]
    v = np.moveaxis(np.asarray(x, np.float32).astype(ml_dtypes.bfloat16).astype(np.float64), axis, -1)
    blocks = v.reshape(v.shape[:-1] + (-1, 32))
    amax = np.abs(blocks).max(-1, keepdims=True)
    byte = np.maximum(np.where(amax > 0, np.frexp(amax)[1] - 1 + 127, 0) - down, 1)
    scale = np.exp2(byte - 127.0)
    codes = (blocks / scale).astype(np.float32).astype(dtype).astype(np.float64)
    return np.moveaxis((codes * scale).reshape(v.shape), -1, axis)


WIDE = False


def mx_kscale(k):
    if not WIDE:
        return np.ones(k)
    levels = np.array([10, -10, 5, -5, 0])
    if k % 512:
        return np.exp2(np.random.permutation(np.resize(levels, k // 32))).repeat(32)
    a = np.empty((k // 512, 16))
    for p in range(k // 512):
        a[p, :8] = np.random.permutation(np.resize(levels, 8))
        for g in range(8):
            far = levels[np.abs(levels - a[p, g]) >= 10]
            a[p, g + 8] = far[np.random.randint(len(far))]
    return np.exp2(a.ravel()).repeat(32)


BF16 = ml_dtypes.bfloat16


def bf(x):
    return np.asarray(x, np.float32).astype(BF16)


def f64(x):
    return np.asarray(x).astype(np.float64)


E2M1 = np.array([0.0, 0.5, 1.0, 1.5, 2.0, 3.0, 4.0, 6.0, -0.0, -0.5, -1.0, -1.5, -2.0, -3.0, -4.0, -6.0])


def pack_weight(w, fmt):
    k, n = w.shape
    w = f64(bf(w)).reshape(k // 32, 32, n)
    amax = np.abs(w).max(1)
    if fmt == "e4m3":
        byte = np.frexp(amax)[1] - 1 + 127 - 7
    else:
        mant, ex = np.frexp(amax / 6.0)
        byte = np.where(mant > 0.5, ex, ex - 1) + 127
    byte = np.clip(np.where(amax > 0, byte, 1), 1, 254)
    scaled = (w * np.exp2(127.0 - byte)[:, None, :]).reshape(k, n).astype(np.float32)
    by_word = np.ascontiguousarray(scaled.reshape(k // 512, 128, 4, n).transpose(0, 1, 3, 2))
    if fmt == "e4m3":
        words = by_word.astype(ml_dtypes.float8_e4m3fn).view(np.uint8)
    else:
        c = by_word.astype(ml_dtypes.float4_e2m1fn).view(np.uint8) & 0xF
        words = c[..., 0::2] | (c[..., 1::2] << 4)
    return np.ascontiguousarray(words), np.ascontiguousarray(byte.astype(np.uint8).reshape(k // 512, 16, n))


def unpack_weight(words, scales, fmt):
    g, p, n, _ = words.shape
    if fmt == "e4m3":
        vals = np.ascontiguousarray(words).view(ml_dtypes.float8_e4m3fn).astype(np.float64)
    else:
        nib = np.empty((g, p, n, 4), np.uint8)
        nib[..., 0::2] = words & 0xF
        nib[..., 1::2] = words >> 4
        vals = E2M1[nib]
    vals = vals * np.repeat(np.exp2(scales.astype(np.float64) - 127.0), 8, axis=1)[..., None]
    return vals.transpose(0, 1, 3, 2).reshape(g * 512, n)
def pack4(w):
    words, scales = pack_weight(w, "e2m1")
    return words.reshape(words.shape[0], 128, -1), scales


def unpack4(words, scales):
    return unpack_weight(words.reshape(words.shape[0], 128, -1, 2), scales, "e2m1")


def planes(Y):
    n, m = Y.shape
    b = f64(bf(Y)).reshape(n // 32, 32, m)
    amax = np.abs(b).max(1)
    byte = np.clip(np.where(amax > 0, np.frexp(amax)[1] - 1 + 127 - 7, 1), 1, 254)
    codes = (b * np.exp2(127.0 - byte)[:, None, :]).reshape(n, m).astype(np.float32).astype(ml_dtypes.float8_e4m3fn).view(np.uint8)
    words = codes.reshape(n // 512, 128, 4, m).transpose(0, 1, 3, 2)
    return np.ascontiguousarray(words), np.ascontiguousarray(byte.astype(np.uint8).reshape(n // 512, 16, m))


STATIONS, TIMES, SENSORS, CHANNELS = 8, 128, 1536, 2048


def setup_inputs():
    s = mx_kscale(SENSORS)
    span = np.exp(0.7 * np.random.randn(CHANNELS))
    x = np.random.randn(SENSORS, STATIONS * TIMES)
    x_words, x_scales = pack_weight(x * s[:, None], "e4m3")
    calibration = np.random.randn(SENSORS, CHANNELS) * span / np.sqrt(SENSORS)
    range_factor = np.exp(0.3 * np.random.randn(STATIONS, TIMES))
    offset = 0.4 * span * np.random.randn(STATIONS, CHANNELS)
    low = -span * (1.0 + 0.5 * np.random.rand(CHANNELS))
    high = span * (1.2 + 0.5 * np.random.rand(CHANNELS))
    return {"x_words": x_words, "x_scales": x_scales,
            "calibration": bf(calibration / s[:, None]),
            "range_factor": bf(range_factor), "offset": bf(offset),
            "low": bf(low), "high": bf(high)}


def reference(x_words, x_scales, calibration, range_factor, offset, low, high):
    x = unpack_weight(x_words, x_scales, "e4m3")
    c = mxq(f64(calibration), 0, "e4m3")
    v = (x.T @ c).reshape(STATIONS, TIMES, CHANNELS)
    v = v * f64(range_factor)[:, :, None] + f64(offset)[:, None, :]
    y = np.minimum(np.maximum(v, f64(low)), f64(high))
    Y = y.reshape(STATIONS * TIMES, CHANNELS).T
    words, scales = planes(Y)
    return y, words, scales

@@ -1,0 +1,271 @@
+from contextlib import ExitStack
+
+import concourse.mybir as mybir
+from concourse.masks import make_identity
+
+F32 = mybir.dt.float32
+BF16 = mybir.dt.bfloat16
+I32 = mybir.dt.int32
+U32 = mybir.dt.uint32
+U8 = mybir.dt.uint8
+FP8X4 = mybir.dt.float8_e4m3fn_x4
+ALU = mybir.AluOpType
+ACT = mybir.ActivationFunctionType
+
+STATIONS, TIMES, SENSORS, CHANNELS = 8, 128, 1536, 2048
+TOKENS = STATIONS * TIMES
+FLOPS = 2 * TOKENS * SENSORS * CHANNELS
+
+P = 128
+PACK = 4
+SPAN = P * PACK
+PASSES = SENSORS // SPAN
+GROUPS = CHANNELS // SPAN
+HALVES = 2
+HALF = TOKENS // HALVES
+HALF_STATIONS = STATIONS // HALVES
+STEPS = GROUPS * HALVES
+VECTOR_M = 64
+LOW_ROW = STATIONS * GROUPS
+HIGH_ROW = LOW_ROW + GROUPS
+PARAM_ROWS = HIGH_ROW + GROUPS
+
+
+def tile_calibrated_clipped_channels_g6_kernel(
+    tc, x_words, x_scales, calibration, range_factor, offset, low, high, out_0, out_1, out_2
+):
+    nc = tc.nc
+    with ExitStack() as ctx:
+        keep = ctx.enter_context(tc.tile_pool(name="keep", bufs=1))
+        work = ctx.enter_context(tc.tile_pool(name="work", bufs=3))
+        psum = ctx.enter_context(tc.psum_pool(name="psum", bufs=1))
+        ctx.enter_context(tc.manual_schedule())
+
+        range_rows = keep.tile([P, TIMES], BF16)
+        x_plane = keep.tile([P, TOKENS], U8, align_bytes=64)
+        param_rows = keep.tile([P, SPAN], BF16)
+        nc.vector.memset(range_rows[:], 0.0)
+        nc.vector.memset(x_plane[:].bitcast(I32), 0)
+        nc.vector.memset(param_rows[:], 0.0)
+        ident = keep.tile([P, P], F32)
+        make_identity(nc, ident[:])
+
+        nc.scalar.dma_start(out=range_rows[0:STATIONS, :], in_=range_factor)
+        for q in range(4):
+            nc.scalar.dma_start(
+                out=x_plane[32 * q : 32 * q + 4 * PASSES, :].bitcast(I32),
+                in_=x_scales[:, 4 * q : 4 * q + 4, :].bitcast(I32),
+            )
+        ident_bf = keep.tile([P, P], BF16)
+        nc.scalar.activation(out=ident_bf[:], in_=ident[:], func=ACT.Identity)
+
+        raw = {}
+
+        def load_calibration(g):
+            for k in range(PASSES):
+                raw[g, k] = keep.tile([P, PACK, SPAN], BF16, name="raw%d_%d" % (g, k))
+                rows = calibration[SPAN * k : SPAN * (k + 1), SPAN * g : SPAN * (g + 1)]
+                nc.sync.dma_start(out=raw[g, k][:], in_=rows.rearrange("(p j) c -> p j c", j=PACK))
+
+        x_codes = {}
+
+        def load_x(h):
+            x_codes[h] = keep.tile([P, PASSES, HALF], U32, name="x_codes%d" % h, align_bytes=64)
+            src = x_words.rearrange("g p n t -> p g (n t)")[:, :, PACK * HALF * h : PACK * HALF * (h + 1)]
+            nc.sync.dma_start(out=x_codes[h][:].bitcast(I32), in_=src.bitcast(I32))
+
+        load_calibration(0)
+        load_x(0)
+        nc.sync.dma_start(out=param_rows[0:LOW_ROW, :], in_=offset.rearrange("s (g c) -> (s g) c", g=GROUPS))
+        nc.sync.dma_start(out=param_rows[LOW_ROW:HIGH_ROW, :], in_=low.rearrange("(g c) -> g c", g=GROUPS))
+        nc.sync.dma_start(out=param_rows[HIGH_ROW:PARAM_ROWS, :], in_=high.rearrange("(g c) -> g c", g=GROUPS))
+        load_x(1)
+        for g in range(1, GROUPS):
+            load_calibration(g)
+
+        grouped = {}
+        w_codes = {}
+        w_plane = {}
+
+        def views(g, k, m0, m1):
+            dst = grouped[g, k][:].rearrange("p (t mm i j) -> p mm t i j", t=PACK, i=2, j=PACK)
+            src = raw[g, k][:].rearrange("p j (mm i t) -> p mm t i j", i=2, t=PACK)
+            return dst[:, m0 // 2 : m1 // 2], src[:, m0 // 2 : m1 // 2]
+
+        def interleave_vector(g, k):
+            grouped[g, k] = work.tile([P, PACK * SPAN], BF16, name="grouped", align_bytes=64, bufs=4)
+            dst, src = views(g, k, 0, VECTOR_M)
+            nc.vector.tensor_copy(out=dst, in_=src)
+
+        def interleave_scalar(g, k):
+            dst, src = views(g, k, VECTOR_M, P)
+            nc.scalar.copy(out=dst, in_=src)
+
+        def quantize_w(g, k):
+            w_codes[g, k] = keep.tile([P, SPAN], U32, name="w_codes%d_%d" % (g, k), align_bytes=64)
+            w_plane[g, k] = keep.tile([P, SPAN], U8, name="w_plane%d_%d" % (g, k), align_bytes=64)
+            nc.vector.quantize_mx(out=w_codes[g, k][:].bitcast(FP8X4), scales=w_plane[g, k][:], in_=grouped[g, k][:])
+
+        acc = {}
+
+        def multiply(u):
+            g, h = divmod(u, HALVES)
+            for t in range(PACK):
+                acc[u, t] = psum.tile([P, HALF], F32, name="acc%d" % t)
+                for k in range(PASSES):
+                    nc.tensor.matmul_mx(
+                        out=acc[u, t][:],
+                        lhsT=w_codes[g, k][:, P * t : P * (t + 1)].bitcast(FP8X4),
+                        lhsT_scale=w_plane[g, k][:, P * t : P * (t + 1)],
+                        rhs=x_codes[h][:, k, :].bitcast(FP8X4),
+                        rhs_scale=x_plane[4 * k : P, HALF * h : HALF * (h + 1)],
+                        start=(k == 0),
+                        stop=(k == PASSES - 1),
+                    )
+
+        range_t = keep.tile([P, STATIONS], BF16)
+        range_all = keep.tile([P, TOKENS], BF16)
+        params = keep.tile([P, PACK, PARAM_ROWS], F32)
+
+        range_ps = psum.tile([P, TIMES], BF16, name="turn0")
+        nc.tensor.transpose(range_ps[:], range_rows[:], ident_bf[:])
+        interleave_vector(0, 0)
+        interleave_scalar(0, 0)
+        nc.vector.tensor_copy(out=range_t[:], in_=range_ps[:, 0:STATIONS])
+        spread_ps = psum.tile([P, TOKENS], BF16, name="turn1")
+        for s in range(STATIONS):
+            nc.tensor.transpose(
+                spread_ps[:, TIMES * s : TIMES * (s + 1)], range_t[:, s : s + 1].to_broadcast([P, P]), ident_bf[:]
+            )
+        interleave_vector(0, 1)
+        interleave_scalar(0, 1)
+        quantize_w(0, 0)
+        interleave_vector(0, 2)
+        interleave_scalar(0, 2)
+        quantize_w(0, 1)
+        nc.vector.tensor_copy(out=range_all[:], in_=spread_ps[:])
+        quantize_w(0, 2)
+        param_ps = psum.tile([P, PACK, P], BF16, name="turn2")
+        for t in range(PACK):
+            nc.tensor.transpose(param_ps[:, t, :], param_rows[:, t:SPAN:PACK], ident_bf[:])
+        nc.scalar.copy(out=params[:], in_=param_ps[:, :, 0:PARAM_ROWS])
+        multiply(0)
+
+        y = {}
+        y_bf = {}
+        turned = {}
+        y_plane = keep.tile([P, TOKENS], U8, align_bytes=64)
+
+        def scale_and_offset(u):
+            g, h = divmod(u, HALVES)
+            y[u] = work.tile([P, PACK, HALF], F32, name="y")
+            for t in range(PACK):
+                nc.vector.tensor_tensor(
+                    out=y[u][:, t, :], in0=acc[u, t][:], in1=range_all[:, HALF * h : HALF * (h + 1)], op=ALU.mult
+                )
+                for i in range(HALF_STATIONS):
+                    row = (HALF_STATIONS * h + i) * GROUPS + g
+                    part = y[u][:, t, TIMES * i : TIMES * (i + 1)]
+                    nc.scalar.activation(out=part, in_=part, func=ACT.Identity, bias=params[:, t, row : row + 1])
+
+        def clip(u, t):
+            g = u // HALVES
+            nc.vector.tensor_scalar(
+                out=y[u][:, t, :],
+                in0=y[u][:, t, :],
+                scalar1=params[:, t, LOW_ROW + g : LOW_ROW + g + 1],
+                scalar2=params[:, t, HIGH_ROW + g : HIGH_ROW + g + 1],
+                op0=ALU.max,
+                op1=ALU.min,
+            )
+
+        def round_y(u, last):
+            y_bf[u] = work.tile([P, HALF * PACK], BF16, name="y_bf", align_bytes=64, bufs=2)
+            dst = y_bf[u][:].rearrange("p (n t) -> p n t", t=PACK)
+            src = y[u][:].rearrange("p t n -> p n t")
+            if last:
+                nc.vector.tensor_copy(out=dst, in_=src)
+            else:
+                nc.gpsimd.tensor_scalar(out=dst, in0=src, scalar1=1.0, scalar2=1.0, op0=ALU.mult, op1=ALU.mult)
+
+        def quantize_y(u):
+            g, h = divmod(u, HALVES)
+            y_codes = work.tile([P, HALF], U32, name="y_codes", align_bytes=64)
+            nc.vector.quantize_mx(
+                out=y_codes[:].bitcast(FP8X4),
+                scales=y_plane[4 * g : P, HALF * h : HALF * (h + 1)],
+                in_=y_bf[u][:],
+            )
+            dst = out_1[g].rearrange("p n t -> p (n t)")[:, PACK * HALF * h : PACK * HALF * (h + 1)]
+            nc.sync.dma_start(out=dst.bitcast(I32), in_=y_codes[:].bitcast(I32))
+
+        def turn(u):
+            for i in range(HALF_STATIONS):
+                turned[u, i] = psum.tile([P, PACK, P], F32, name="turn%d" % i)
+                for t in range(PACK):
+                    nc.tensor.transpose(turned[u, i][:, t, :], y[u][:, t, TIMES * i : TIMES * (i + 1)], ident[:])
+
+        def store_y(u, i):
+            g, h = divmod(u, HALVES)
+            rows = work.tile([P, SPAN], F32, name="rows", bufs=8)
+            dst = rows[:].rearrange("p (m t) -> p m t", t=PACK)
+            src = turned[u, i][:].rearrange("p t m -> p m t")
+            if i == HALF_STATIONS - 1:
+                nc.vector.tensor_copy(out=dst, in_=src)
+            else:
+                nc.scalar.copy(out=dst, in_=src)
+            nc.sync.dma_start(out=out_0[HALF_STATIONS * h + i, :, SPAN * g : SPAN * (g + 1)], in_=rows[:])
+
+        def to_interleave(u):
+            if u == 0:
+                return [(1, k) for k in range(PASSES)]
+            g = (u + 3) // 2
+            if g >= GROUPS:
+                return []
+            return [(g, 0), (g, 1)] if u % 2 else [(g, 2)]
+
+        for u in range(STEPS):
+            if u > 0:
+                round_y(u - 1, False)
+                turn(u - 1)
+            scale_and_offset(u)
+            blocks = to_interleave(u)
+            if u > 0:
+                store_y(u - 1, HALF_STATIONS - 1)
+            nxt = u // 2 + 1
+            if u % 2 == 1 and nxt < GROUPS:
+                quantize_w(nxt, 2)
+            if u + 1 < STEPS:
+                multiply(u + 1)
+            if u % 2 == 0 and 0 < u and nxt < GROUPS:
+                quantize_w(nxt, 0)
+            for b in blocks:
+                interleave_vector(*b)
+            if blocks:
+                interleave_scalar(*blocks[0])
+            if u > 0:
+                quantize_y(u - 1)
+                for i in range(HALF_STATIONS - 1):
+                    store_y(u - 1, i)
+            for b in blocks[1:]:
+                interleave_scalar(*b)
+            clip(u, 0)
+            clip(u, 1)
+            if u == 0:
+                quantize_w(1, 0)
+            clip(u, 2)
+            if u % 2 == 0 and nxt < GROUPS:
+                quantize_w(nxt, 1)
+            clip(u, 3)
+
+        last = STEPS - 1
+        turn(last)
+        round_y(last, True)
+        for i in range(HALF_STATIONS):
+            store_y(last, i)
+        quantize_y(last)
+        for q in range(4):
+            nc.sync.dma_start(
+                out=out_2[:, 4 * q : 4 * q + 4, :].bitcast(I32),
+                in_=y_plane[32 * q : 32 * q + 4 * GROUPS, :].bitcast(I32),
+            )

@@ -25,7 +25,13 @@ HALVES = 2
 HALF = TOKENS // HALVES
 HALF_STATIONS = STATIONS // HALVES
 STEPS = GROUPS * HALVES
-VECTOR_M = 64
+VECTOR_M = (16, 56, 56)
+VECTOR_M_SECOND = 64
+VECTOR_M_FIRST = 72
+GPSIMD_TOKENS = 448
+VECTOR_STORES = 1
+GPSIMD_STATIONS = 2
+UNITS = [(g, s0, 4) for g in range(GROUPS - 1) for s0 in (0, 4)] + [(GROUPS - 1, s0, n) for s0, n in [(0, 4), (4, 2), (6, 2)]]
 LOW_ROW = STATIONS * GROUPS
 HIGH_ROW = LOW_ROW + GROUPS
 PARAM_ROWS = HIGH_ROW + GROUPS
@@ -42,46 +48,53 @@ def tile_calibrated_clipped_channels_g6_kernel(
         ctx.enter_context(tc.manual_schedule())
 
         range_rows = keep.tile([P, TIMES], BF16)
-        x_plane = keep.tile([P, TOKENS], U8, align_bytes=64)
+        x_plane = keep.tile([P, PASSES, TOKENS], U8, align_bytes=64)
         param_rows = keep.tile([P, SPAN], BF16)
         nc.vector.memset(range_rows[:], 0.0)
-        nc.vector.memset(x_plane[:].bitcast(I32), 0)
         nc.vector.memset(param_rows[:], 0.0)
+        nc.vector.memset(x_plane[:].rearrange("p k n -> p (k n)").bitcast(I32), 0)
         ident = keep.tile([P, P], F32)
         make_identity(nc, ident[:])
 
         nc.scalar.dma_start(out=range_rows[0:STATIONS, :], in_=range_factor)
-        for q in range(4):
-            nc.scalar.dma_start(
-                out=x_plane[32 * q : 32 * q + 4 * PASSES, :].bitcast(I32),
-                in_=x_scales[:, 4 * q : 4 * q + 4, :].bitcast(I32),
-            )
+        nc.scalar.dma_start(out=param_rows[0:LOW_ROW, :], in_=offset.rearrange("s (g c) -> (s g) c", g=GROUPS))
+        nc.scalar.dma_start(out=param_rows[LOW_ROW:HIGH_ROW, :], in_=low.rearrange("(g c) -> g c", g=GROUPS))
+        nc.scalar.dma_start(out=param_rows[HIGH_ROW:PARAM_ROWS, :], in_=high.rearrange("(g c) -> g c", g=GROUPS))
         ident_bf = keep.tile([P, P], BF16)
         nc.scalar.activation(out=ident_bf[:], in_=ident[:], func=ACT.Identity)
 
         raw = {}
 
-        def load_calibration(g):
-            for k in range(PASSES):
-                raw[g, k] = keep.tile([P, PACK, SPAN], BF16, name="raw%d_%d" % (g, k))
-                rows = calibration[SPAN * k : SPAN * (k + 1), SPAN * g : SPAN * (g + 1)]
-                nc.sync.dma_start(out=raw[g, k][:], in_=rows.rearrange("(p j) c -> p j c", j=PACK))
+        def load_w(g, k):
+            raw[g, k] = keep.tile([P, PACK, SPAN], BF16, name="raw%d_%d" % (g, k))
+            rows = calibration[SPAN * k : SPAN * (k + 1), SPAN * g : SPAN * (g + 1)]
+            nc.sync.dma_start(out=raw[g, k][:], in_=rows.rearrange("(p j) c -> p j c", j=PACK))
 
         x_codes = {}
 
-        def load_x(h):
-            x_codes[h] = keep.tile([P, PASSES, HALF], U32, name="x_codes%d" % h, align_bytes=64)
-            src = x_words.rearrange("g p n t -> p g (n t)")[:, :, PACK * HALF * h : PACK * HALF * (h + 1)]
-            nc.sync.dma_start(out=x_codes[h][:].bitcast(I32), in_=src.bitcast(I32))
+        def load_x(h, k):
+            x_codes[h, k] = keep.tile([P, HALF], U32, name="x_codes%d_%d" % (h, k), align_bytes=64)
+            src = x_words[k].rearrange("p n t -> p (n t)")[:, PACK * HALF * h : PACK * HALF * (h + 1)]
+            nc.sync.dma_start(out=x_codes[h, k][:].bitcast(I32), in_=src.bitcast(I32))
 
-        load_calibration(0)
-        load_x(0)
-        nc.sync.dma_start(out=param_rows[0:LOW_ROW, :], in_=offset.rearrange("s (g c) -> (s g) c", g=GROUPS))
-        nc.sync.dma_start(out=param_rows[LOW_ROW:HIGH_ROW, :], in_=low.rearrange("(g c) -> g c", g=GROUPS))
-        nc.sync.dma_start(out=param_rows[HIGH_ROW:PARAM_ROWS, :], in_=high.rearrange("(g c) -> g c", g=GROUPS))
-        load_x(1)
+        load_w(0, 0)
+        load_x(0, 0)
+        load_w(0, 1)
+        load_w(0, 2)
+        for q in range(4):
+            nc.sync.dma_start(
+                out=x_plane[32 * q : 32 * q + 4, :, :].bitcast(I32),
+                in_=x_scales[:, 4 * q : 4 * q + 4, :].rearrange("k r n -> r k n").bitcast(I32),
+            )
+        load_x(0, 1)
+        load_x(0, 2)
+        load_w(1, 0)
+        for k in range(PASSES):
+            load_x(1, k)
         for g in range(1, GROUPS):
-            load_calibration(g)
+            for k in range(PASSES):
+                if (g, k) not in raw:
+                    load_w(g, k)
 
         grouped = {}
         w_codes = {}
@@ -92,13 +105,19 @@ def tile_calibrated_clipped_channels_g6_kernel(
             src = raw[g, k][:].rearrange("p j (mm i t) -> p mm t i j", i=2, t=PACK)
             return dst[:, m0 // 2 : m1 // 2], src[:, m0 // 2 : m1 // 2]
 
+        def split(g, k):
+            if (g, k) not in grouped:
+                grouped[g, k] = work.tile([P, PACK * SPAN], BF16, name="grouped", align_bytes=64, bufs=4)
+            return VECTOR_M_FIRST if g == 0 else VECTOR_M[k]
+
         def interleave_vector(g, k):
-            grouped[g, k] = work.tile([P, PACK * SPAN], BF16, name="grouped", align_bytes=64, bufs=4)
-            dst, src = views(g, k, 0, VECTOR_M)
+            m = split(g, k)
+            dst, src = views(g, k, 0, m)
             nc.vector.tensor_copy(out=dst, in_=src)
 
         def interleave_scalar(g, k):
-            dst, src = views(g, k, VECTOR_M, P)
+            m = split(g, k)
+            dst, src = views(g, k, m, P)
             nc.scalar.copy(out=dst, in_=src)
 
         def quantize_w(g, k):
@@ -108,20 +127,21 @@ def tile_calibrated_clipped_channels_g6_kernel(
 
         acc = {}
 
-        def multiply(u):
-            g, h = divmod(u, HALVES)
-            for t in range(PACK):
-                acc[u, t] = psum.tile([P, HALF], F32, name="acc%d" % t)
-                for k in range(PASSES):
-                    nc.tensor.matmul_mx(
-                        out=acc[u, t][:],
-                        lhsT=w_codes[g, k][:, P * t : P * (t + 1)].bitcast(FP8X4),
-                        lhsT_scale=w_plane[g, k][:, P * t : P * (t + 1)],
-                        rhs=x_codes[h][:, k, :].bitcast(FP8X4),
-                        rhs_scale=x_plane[4 * k : P, HALF * h : HALF * (h + 1)],
-                        start=(k == 0),
-                        stop=(k == PASSES - 1),
-                    )
+        def multiply(u, t, passes):
+            g, s0, n = UNITS[u]
+            h, c0 = divmod(TIMES * s0, HALF)
+            for k in passes:
+                if k == 0:
+                    acc[u, t] = psum.tile([P, TIMES * n], F32, name="acc%d" % t)
+                nc.tensor.matmul_mx(
+                    out=acc[u, t][:],
+                    lhsT=w_codes[g, k][:, P * t : P * (t + 1)].bitcast(FP8X4),
+                    lhsT_scale=w_plane[g, k][:, P * t : P * (t + 1)],
+                    rhs=x_codes[h, k][:, c0 : c0 + TIMES * n].bitcast(FP8X4),
+                    rhs_scale=x_plane[:, k, TIMES * s0 : TIMES * (s0 + n)],
+                    start=(k == 0),
+                    stop=(k == PASSES - 1),
+                )
 
         range_t = keep.tile([P, STATIONS], BF16)
         range_all = keep.tile([P, TOKENS], BF16)
@@ -129,47 +149,53 @@ def tile_calibrated_clipped_channels_g6_kernel(
 
         range_ps = psum.tile([P, TIMES], BF16, name="turn0")
         nc.tensor.transpose(range_ps[:], range_rows[:], ident_bf[:])
-        interleave_vector(0, 0)
-        interleave_scalar(0, 0)
         nc.vector.tensor_copy(out=range_t[:], in_=range_ps[:, 0:STATIONS])
+        param_ps = psum.tile([P, PACK, P], BF16, name="turn2")
+        for t in range(PACK):
+            nc.tensor.transpose(param_ps[:, t, :], param_rows[:, t:SPAN:PACK], ident_bf[:])
         spread_ps = psum.tile([P, TOKENS], BF16, name="turn1")
         for s in range(STATIONS):
             nc.tensor.transpose(
                 spread_ps[:, TIMES * s : TIMES * (s + 1)], range_t[:, s : s + 1].to_broadcast([P, P]), ident_bf[:]
             )
+        interleave_vector(0, 0)
+        interleave_scalar(0, 0)
+        nc.vector.tensor_copy(out=params[:], in_=param_ps[:, :, 0:PARAM_ROWS])
+        quantize_w(0, 0)
+        for t in range(PACK):
+            multiply(0, t, [0])
         interleave_vector(0, 1)
         interleave_scalar(0, 1)
-        quantize_w(0, 0)
+        nc.vector.tensor_copy(out=range_all[:], in_=spread_ps[:])
+        quantize_w(0, 1)
         interleave_vector(0, 2)
         interleave_scalar(0, 2)
-        quantize_w(0, 1)
-        nc.vector.tensor_copy(out=range_all[:], in_=spread_ps[:])
-        quantize_w(0, 2)
-        param_ps = psum.tile([P, PACK, P], BF16, name="turn2")
         for t in range(PACK):
-            nc.tensor.transpose(param_ps[:, t, :], param_rows[:, t:SPAN:PACK], ident_bf[:])
-        nc.scalar.copy(out=params[:], in_=param_ps[:, :, 0:PARAM_ROWS])
-        multiply(0)
+            multiply(0, t, [1])
+        quantize_w(0, 2)
+        for t in range(PACK):
+            multiply(0, t, [2])
+        interleave_scalar(1, 0)
 
         y = {}
         y_bf = {}
         turned = {}
         y_plane = keep.tile([P, TOKENS], U8, align_bytes=64)
 
-        def scale_and_offset(u):
-            g, h = divmod(u, HALVES)
-            y[u] = work.tile([P, PACK, HALF], F32, name="y")
-            for t in range(PACK):
-                nc.vector.tensor_tensor(
-                    out=y[u][:, t, :], in0=acc[u, t][:], in1=range_all[:, HALF * h : HALF * (h + 1)], op=ALU.mult
-                )
-                for i in range(HALF_STATIONS):
-                    row = (HALF_STATIONS * h + i) * GROUPS + g
-                    part = y[u][:, t, TIMES * i : TIMES * (i + 1)]
-                    nc.scalar.activation(out=part, in_=part, func=ACT.Identity, bias=params[:, t, row : row + 1])
+        def scale_and_offset(u, t):
+            g, s0, n = UNITS[u]
+            if t == 0:
+                y[u] = work.tile([P, PACK, TIMES * n], F32, name="y")
+            nc.vector.tensor_tensor(
+                out=y[u][:, t, :], in0=acc[u, t][:], in1=range_all[:, TIMES * s0 : TIMES * (s0 + n)], op=ALU.mult
+            )
+            for i in range(n):
+                row = (s0 + i) * GROUPS + g
+                part = y[u][:, t, TIMES * i : TIMES * (i + 1)]
+                nc.scalar.activation(out=part, in_=part, func=ACT.Identity, bias=params[:, t, row : row + 1])
 
         def clip(u, t):
-            g = u // HALVES
+            g = UNITS[u][0]
             nc.vector.tensor_scalar(
                 out=y[u][:, t, :],
                 in0=y[u][:, t, :],
@@ -179,93 +205,112 @@ def tile_calibrated_clipped_channels_g6_kernel(
                 op1=ALU.min,
             )
 
-        def round_y(u, last):
-            y_bf[u] = work.tile([P, HALF * PACK], BF16, name="y_bf", align_bytes=64, bufs=2)
-            dst = y_bf[u][:].rearrange("p (n t) -> p n t", t=PACK)
-            src = y[u][:].rearrange("p t n -> p n t")
-            if last:
-                nc.vector.tensor_copy(out=dst, in_=src)
-            else:
+        def round_y(u, n0, n1, engine):
+            if n0 == 0:
+                y_bf[u] = work.tile([P, TIMES * UNITS[u][2] * PACK], BF16, name="y_bf", align_bytes=64, bufs=6)
+            dst = y_bf[u][:].rearrange("p (n t) -> p n t", t=PACK)[:, n0:n1]
+            src = y[u][:].rearrange("p t n -> p n t")[:, n0:n1]
+            if engine == "gpsimd":
                 nc.gpsimd.tensor_scalar(out=dst, in0=src, scalar1=1.0, scalar2=1.0, op0=ALU.mult, op1=ALU.mult)
+            elif engine == "scalar":
+                nc.scalar.copy(out=dst, in_=src)
+            else:
+                nc.vector.tensor_copy(out=dst, in_=src)
 
         def quantize_y(u):
-            g, h = divmod(u, HALVES)
-            y_codes = work.tile([P, HALF], U32, name="y_codes", align_bytes=64)
+            g, s0, n = UNITS[u]
+            y_codes = work.tile([P, TIMES * n], U32, name="y_codes", align_bytes=64)
             nc.vector.quantize_mx(
                 out=y_codes[:].bitcast(FP8X4),
-                scales=y_plane[4 * g : P, HALF * h : HALF * (h + 1)],
+                scales=y_plane[4 * g : P, TIMES * s0 : TIMES * (s0 + n)],
                 in_=y_bf[u][:],
             )
-            dst = out_1[g].rearrange("p n t -> p (n t)")[:, PACK * HALF * h : PACK * HALF * (h + 1)]
+            dst = out_1[g].rearrange("p n t -> p (n t)")[:, PACK * TIMES * s0 : PACK * TIMES * (s0 + n)]
             nc.sync.dma_start(out=dst.bitcast(I32), in_=y_codes[:].bitcast(I32))
 
-        def turn(u):
-            for i in range(HALF_STATIONS):
-                turned[u, i] = psum.tile([P, PACK, P], F32, name="turn%d" % i)
-                for t in range(PACK):
-                    nc.tensor.transpose(turned[u, i][:, t, :], y[u][:, t, TIMES * i : TIMES * (i + 1)], ident[:])
+        def store_scales(n0, n1):
+            for q in range(4):
+                nc.sync.dma_start(
+                    out=out_2[:, 4 * q : 4 * q + 4, n0:n1].bitcast(I32),
+                    in_=y_plane[32 * q : 32 * q + 4 * GROUPS, n0:n1].bitcast(I32),
+                )
 
-        def store_y(u, i):
-            g, h = divmod(u, HALVES)
+        def turn(u, i, t):
+            s0 = UNITS[u][1]
+            if t == 0:
+                turned[u, i] = psum.tile([P, PACK, P], F32, name="turn%d" % ((s0 + i) % 4))
+            nc.tensor.transpose(turned[u, i][:, t, :], y[u][:, t, TIMES * i : TIMES * (i + 1)], ident[:])
+
+        def store_y(u, i, on_vector):
+            g, s0, n = UNITS[u]
             rows = work.tile([P, SPAN], F32, name="rows", bufs=8)
             dst = rows[:].rearrange("p (m t) -> p m t", t=PACK)
             src = turned[u, i][:].rearrange("p t m -> p m t")
-            if i == HALF_STATIONS - 1:
+            if on_vector:
                 nc.vector.tensor_copy(out=dst, in_=src)
             else:
                 nc.scalar.copy(out=dst, in_=src)
-            nc.sync.dma_start(out=out_0[HALF_STATIONS * h + i, :, SPAN * g : SPAN * (g + 1)], in_=rows[:])
+            nc.sync.dma_start(out=out_0[s0 + i, :, SPAN * g : SPAN * (g + 1)], in_=rows[:])
 
-        def to_interleave(u):
-            if u == 0:
-                return [(1, k) for k in range(PASSES)]
-            g = (u + 3) // 2
-            if g >= GROUPS:
-                return []
-            return [(g, 0), (g, 1)] if u % 2 else [(g, 2)]
-
-        for u in range(STEPS):
-            if u > 0:
-                round_y(u - 1, False)
-                turn(u - 1)
-            scale_and_offset(u)
-            blocks = to_interleave(u)
-            if u > 0:
-                store_y(u - 1, HALF_STATIONS - 1)
-            nxt = u // 2 + 1
-            if u % 2 == 1 and nxt < GROUPS:
-                quantize_w(nxt, 2)
-            if u + 1 < STEPS:
-                multiply(u + 1)
-            if u % 2 == 0 and 0 < u and nxt < GROUPS:
-                quantize_w(nxt, 0)
-            for b in blocks:
-                interleave_vector(*b)
-            if blocks:
-                interleave_scalar(*blocks[0])
-            if u > 0:
+        last = len(UNITS) - 1
+        for u in range(last + 1):
+            g, s0, n = UNITS[u]
+            before = UNITS[u - 1][2] if u > 0 else 0
+            full = n == HALF_STATIONS
+            shared = min(GPSIMD_TOKENS if full else 256, TIMES * before) if before >= GPSIMD_STATIONS else 0
+            on_vector = VECTOR_STORES if full else 1
+            new_group = u < last and UNITS[u + 1][0] != g
+            early = g + 1 < GROUPS and not new_group
+            if shared:
+                round_y(u - 1, 0, shared, "gpsimd")
+            for t in range(PACK):
+                if t < before:
+                    for tt in range(PACK):
+                        turn(u - 1, t, tt)
+                scale_and_offset(u, t)
+                if u < last:
+                    multiply(u + 1, t, [0] if new_group else [0, 1, 2])
+            for i in range(min(before, on_vector)):
+                store_y(u - 1, i, True)
+            if shared < TIMES * before:
+                round_y(u - 1, shared, TIMES * before, "vector")
+            if early:
+                interleave_vector(g + 1, 0)
+                interleave_vector(g + 1, 1)
+            elif new_group:
+                interleave_vector(g + 1, 2)
+                quantize_w(g + 1, 1)
+                for t in range(PACK):
+                    multiply(u + 1, t, [1])
+            else:
+                clip(u, 0)
+            if before:
                 quantize_y(u - 1)
-                for i in range(HALF_STATIONS - 1):
-                    store_y(u - 1, i)
-            for b in blocks[1:]:
-                interleave_scalar(*b)
-            clip(u, 0)
-            clip(u, 1)
-            if u == 0:
-                quantize_w(1, 0)
-            clip(u, 2)
-            if u % 2 == 0 and nxt < GROUPS:
-                quantize_w(nxt, 1)
-            clip(u, 3)
+            if u == last - 1:
+                store_scales(0, HALF)
+            for i in range(on_vector, before):
+                store_y(u - 1, i, False)
+            if early:
+                interleave_scalar(g + 1, 1)
+                interleave_scalar(g + 1, 2)
+            elif new_group and g + 2 < GROUPS:
+                interleave_scalar(g + 2, 0)
+            for t in range(PACK):
+                if t == 1 and early:
+                    quantize_w(g + 1, 0)
+                if t == 1 and new_group:
+                    quantize_w(g + 1, 2)
+                    for tt in range(PACK):
+                        multiply(u + 1, tt, [2])
+                if early or new_group or t > 0:
+                    clip(u, t)
+                if u == last:
+                    for i in range(n):
+                        turn(u, i, t)
 
-        last = STEPS - 1
-        turn(last)
-        round_y(last, True)
-        for i in range(HALF_STATIONS):
-            store_y(last, i)
+        round_y(last, 0, TIMES * UNITS[last][2] - 64, "vector")
+        round_y(last, TIMES * UNITS[last][2] - 64, TIMES * UNITS[last][2], "scalar")
+        store_y(last, 0, False)
         quantize_y(last)
-        for q in range(4):
-            nc.sync.dma_start(
-                out=out_2[:, 4 * q : 4 * q + 4, :].bitcast(I32),
-                in_=y_plane[32 * q : 32 * q + 4 * GROUPS, :].bitcast(I32),
-            )
+        store_y(last, 1, False)
+        store_scales(HALF, TOKENS)

@@ -25,10 +25,10 @@ HALVES = 2
 HALF = TOKENS // HALVES
 HALF_STATIONS = STATIONS // HALVES
 STEPS = GROUPS * HALVES
-VECTOR_M = (16, 56, 56)
+VECTOR_M = (24, 48, 48)
 VECTOR_M_SECOND = 64
 VECTOR_M_FIRST = 72
-GPSIMD_TOKENS = 448
+GPSIMD_TOKENS = 416
 VECTOR_STORES = 1
 GPSIMD_STATIONS = 2
 UNITS = [(g, s0, 4) for g in range(GROUPS - 1) for s0 in (0, 4)] + [(GROUPS - 1, s0, n) for s0, n in [(0, 4), (4, 2), (6, 2)]]
@@ -101,8 +101,8 @@ def tile_calibrated_clipped_channels_g6_kernel(
         w_plane = {}
 
         def views(g, k, m0, m1):
-            dst = grouped[g, k][:].rearrange("p (t mm i j) -> p mm t i j", t=PACK, i=2, j=PACK)
-            src = raw[g, k][:].rearrange("p j (mm i t) -> p mm t i j", i=2, t=PACK)
+            dst = grouped[g, k][:].rearrange("p (t mm i j) -> p mm t j i", t=PACK, i=2, j=PACK)
+            src = raw[g, k][:].rearrange("p j (mm i t) -> p mm t j i", i=2, t=PACK)
             return dst[:, m0 // 2 : m1 // 2], src[:, m0 // 2 : m1 // 2]
 
         def split(g, k):
@@ -208,8 +208,8 @@ def tile_calibrated_clipped_channels_g6_kernel(
         def round_y(u, n0, n1, engine):
             if n0 == 0:
                 y_bf[u] = work.tile([P, TIMES * UNITS[u][2] * PACK], BF16, name="y_bf", align_bytes=64, bufs=6)
-            dst = y_bf[u][:].rearrange("p (n t) -> p n t", t=PACK)[:, n0:n1]
-            src = y[u][:].rearrange("p t n -> p n t")[:, n0:n1]
+            dst = y_bf[u][:].rearrange("p (n i t) -> p n t i", i=2, t=PACK)[:, n0 // 2 : n1 // 2]
+            src = y[u][:].rearrange("p t (n i) -> p n t i", i=2)[:, n0 // 2 : n1 // 2]
             if engine == "gpsimd":
                 nc.gpsimd.tensor_scalar(out=dst, in0=src, scalar1=1.0, scalar2=1.0, op0=ALU.mult, op1=ALU.mult)
             elif engine == "scalar":
@@ -257,7 +257,7 @@ def tile_calibrated_clipped_channels_g6_kernel(
             g, s0, n = UNITS[u]
             before = UNITS[u - 1][2] if u > 0 else 0
             full = n == HALF_STATIONS
-            shared = min(GPSIMD_TOKENS if full else 256, TIMES * before) if before >= GPSIMD_STATIONS else 0
+            shared = min(GPSIMD_TOKENS if full else 224, TIMES * before) if before >= GPSIMD_STATIONS else 0
             on_vector = VECTOR_STORES if full else 1
             new_group = u < last and UNITS[u + 1][0] != g
             early = g + 1 < GROUPS and not new_group
@@ -284,10 +284,8 @@ def tile_calibrated_clipped_channels_g6_kernel(
                     multiply(u + 1, t, [1])
             else:
                 clip(u, 0)
-            if before:
+            if u == last:
                 quantize_y(u - 1)
-            if u == last - 1:
-                store_scales(0, HALF)
             for i in range(on_vector, before):
                 store_y(u - 1, i, False)
             if early:
@@ -296,7 +294,7 @@ def tile_calibrated_clipped_channels_g6_kernel(
             elif new_group and g + 2 < GROUPS:
                 interleave_scalar(g + 2, 0)
             for t in range(PACK):
-                if t == 1 and early:
+                if t == 1 and early and u > 0:
                     quantize_w(g + 1, 0)
                 if t == 1 and new_group:
                     quantize_w(g + 1, 2)
@@ -307,6 +305,12 @@ def tile_calibrated_clipped_channels_g6_kernel(
                 if u == last:
                     for i in range(n):
                         turn(u, i, t)
+            if u == 0:
+                quantize_w(1, 0)
+            elif u < last:
+                quantize_y(u - 1)
+            if u == last - 1:
+                store_scales(0, HALF)
 
         round_y(last, 0, TIMES * UNITS[last][2] - 64, "vector")
         round_y(last, TIMES * UNITS[last][2] - 64, TIMES * UNITS[last][2], "scalar")

@@ -18,23 +18,26 @@ FLOPS = 2 * TOKENS * SENSORS * CHANNELS
 
 P = 128
 PACK = 4
+QUADRANTS = 4
 SPAN = P * PACK
 PASSES = SENSORS // SPAN
 GROUPS = CHANNELS // SPAN
-HALVES = 2
-HALF = TOKENS // HALVES
-HALF_STATIONS = STATIONS // HALVES
-STEPS = GROUPS * HALVES
-VECTOR_M = (24, 48, 48)
-VECTOR_M_SECOND = 64
-VECTOR_M_FIRST = 72
-GPSIMD_TOKENS = 416
-VECTOR_STORES = 1
-GPSIMD_STATIONS = 2
-UNITS = [(g, s0, 4) for g in range(GROUPS - 1) for s0 in (0, 4)] + [(GROUPS - 1, s0, n) for s0, n in [(0, 4), (4, 2), (6, 2)]]
+HALF = TOKENS // 2
+HALF_STATIONS = STATIONS // 2
+
+UNITS = [(g, s, HALF_STATIONS) for g in range(GROUPS) for s in (0, HALF_STATIONS)][:-1]
+UNITS = UNITS + [(GROUPS - 1, s, 2) for s in (HALF_STATIONS, HALF_STATIONS + 2)]
+LAST = len(UNITS) - 1
+
+VECTOR_COLUMNS_FIRST = 64
+VECTOR_COLUMNS = (24, 48, 48)
+GPSIMD_TOKENS_PER_STATION = 80
+GPSIMD_TOKENS_PER_BANK = 96
+SCALAR_LAST_TOKENS = 96
+
 LOW_ROW = STATIONS * GROUPS
 HIGH_ROW = LOW_ROW + GROUPS
-PARAM_ROWS = HIGH_ROW + GROUPS
+CONSTANT_ROWS = HIGH_ROW + GROUPS
 
 
 def tile_calibrated_clipped_channels_g6_kernel(
@@ -49,169 +52,175 @@ def tile_calibrated_clipped_channels_g6_kernel(
 
         range_rows = keep.tile([P, TIMES], BF16)
         x_plane = keep.tile([P, PASSES, TOKENS], U8, align_bytes=64)
-        param_rows = keep.tile([P, SPAN], BF16)
+        constant_rows = keep.tile([P, SPAN], BF16)
         nc.vector.memset(range_rows[:], 0.0)
-        nc.vector.memset(param_rows[:], 0.0)
+        nc.vector.memset(constant_rows[:], 0.0)
         nc.vector.memset(x_plane[:].rearrange("p k n -> p (k n)").bitcast(I32), 0)
         ident = keep.tile([P, P], F32)
         make_identity(nc, ident[:])
 
         nc.scalar.dma_start(out=range_rows[0:STATIONS, :], in_=range_factor)
-        nc.scalar.dma_start(out=param_rows[0:LOW_ROW, :], in_=offset.rearrange("s (g c) -> (s g) c", g=GROUPS))
-        nc.scalar.dma_start(out=param_rows[LOW_ROW:HIGH_ROW, :], in_=low.rearrange("(g c) -> g c", g=GROUPS))
-        nc.scalar.dma_start(out=param_rows[HIGH_ROW:PARAM_ROWS, :], in_=high.rearrange("(g c) -> g c", g=GROUPS))
+        nc.scalar.dma_start(out=constant_rows[0:LOW_ROW, :], in_=offset.rearrange("s (g c) -> (s g) c", g=GROUPS))
+        nc.scalar.dma_start(out=constant_rows[LOW_ROW:HIGH_ROW, :], in_=low.rearrange("(g c) -> g c", g=GROUPS))
+        nc.scalar.dma_start(out=constant_rows[HIGH_ROW:CONSTANT_ROWS, :], in_=high.rearrange("(g c) -> g c", g=GROUPS))
         ident_bf = keep.tile([P, P], BF16)
         nc.scalar.activation(out=ident_bf[:], in_=ident[:], func=ACT.Identity)
 
-        raw = {}
-
-        def load_w(g, k):
-            raw[g, k] = keep.tile([P, PACK, SPAN], BF16, name="raw%d_%d" % (g, k))
-            rows = calibration[SPAN * k : SPAN * (k + 1), SPAN * g : SPAN * (g + 1)]
-            nc.sync.dma_start(out=raw[g, k][:], in_=rows.rearrange("(p j) c -> p j c", j=PACK))
-
+        slab = {}
         x_codes = {}
+
+        def load_slab(g, k):
+            slab[g, k] = keep.tile([P, PACK, SPAN], BF16, name="slab%d_%d" % (g, k))
+            part = calibration[SPAN * k : SPAN * (k + 1), SPAN * g : SPAN * (g + 1)]
+            nc.sync.dma_start(out=slab[g, k][:], in_=part.rearrange("(p j) c -> p j c", j=PACK))
 
         def load_x(h, k):
             x_codes[h, k] = keep.tile([P, HALF], U32, name="x_codes%d_%d" % (h, k), align_bytes=64)
-            src = x_words[k].rearrange("p n t -> p (n t)")[:, PACK * HALF * h : PACK * HALF * (h + 1)]
-            nc.sync.dma_start(out=x_codes[h, k][:].bitcast(I32), in_=src.bitcast(I32))
+            part = x_words[k].rearrange("p n j -> p (n j)")[:, PACK * HALF * h : PACK * HALF * (h + 1)]
+            nc.sync.dma_start(out=x_codes[h, k][:].bitcast(I32), in_=part.bitcast(I32))
 
-        load_w(0, 0)
+        load_slab(0, 0)
         load_x(0, 0)
-        load_w(0, 1)
-        load_w(0, 2)
-        for q in range(4):
+        load_slab(0, 1)
+        load_slab(0, 2)
+        for q in range(QUADRANTS):
             nc.sync.dma_start(
                 out=x_plane[32 * q : 32 * q + 4, :, :].bitcast(I32),
                 in_=x_scales[:, 4 * q : 4 * q + 4, :].rearrange("k r n -> r k n").bitcast(I32),
             )
         load_x(0, 1)
         load_x(0, 2)
-        load_w(1, 0)
+        load_slab(1, 0)
         for k in range(PASSES):
             load_x(1, k)
         for g in range(1, GROUPS):
             for k in range(PASSES):
-                if (g, k) not in raw:
-                    load_w(g, k)
+                if (g, k) not in slab:
+                    load_slab(g, k)
 
-        grouped = {}
+        mixed = {}
         w_codes = {}
         w_plane = {}
+        product = {}
 
-        def views(g, k, m0, m1):
-            dst = grouped[g, k][:].rearrange("p (t mm i j) -> p mm t j i", t=PACK, i=2, j=PACK)
-            src = raw[g, k][:].rearrange("p j (mm i t) -> p mm t j i", i=2, t=PACK)
-            return dst[:, m0 // 2 : m1 // 2], src[:, m0 // 2 : m1 // 2]
+        def interleave(g, k, engine):
+            if (g, k) not in mixed:
+                if (g, k) in ((0, PASSES - 1), (1, 0)):
+                    mixed[g, k] = keep.tile([P, PACK * SPAN], BF16, name="mixed_shared", align_bytes=64)
+                else:
+                    mixed[g, k] = work.tile([P, PACK * SPAN], BF16, name="mixed", align_bytes=64, bufs=4)
+            split = VECTOR_COLUMNS_FIRST if g == 0 else VECTOR_COLUMNS[k]
+            if engine == "gpsimd":
+                dst = mixed[g, k][:].rearrange("p (t m j) -> p m t j", t=PACK, j=PACK)[:, split:P]
+                src = slab[g, k][:].rearrange("p j (m t) -> p m t j", t=PACK)[:, split:P]
+                copy_on_gpsimd(dst, src)
+                return
+            dst = mixed[g, k][:].rearrange("p (t m i j) -> p m t j i", t=PACK, i=2, j=PACK)
+            src = slab[g, k][:].rearrange("p j (m i t) -> p m t j i", i=2, t=PACK)
+            if engine == "vector":
+                nc.vector.tensor_copy(out=dst[:, 0 : split // 2], in_=src[:, 0 : split // 2])
+            else:
+                nc.scalar.copy(out=dst[:, split // 2 : P // 2], in_=src[:, split // 2 : P // 2])
 
-        def split(g, k):
-            if (g, k) not in grouped:
-                grouped[g, k] = work.tile([P, PACK * SPAN], BF16, name="grouped", align_bytes=64, bufs=4)
-            return VECTOR_M_FIRST if g == 0 else VECTOR_M[k]
+        def copy_on_gpsimd(dst, src):
+            nc.gpsimd.tensor_scalar(out=dst, in0=src, scalar1=1.0, scalar2=1.0, op0=ALU.mult, op1=ALU.mult)
 
-        def interleave_vector(g, k):
-            m = split(g, k)
-            dst, src = views(g, k, 0, m)
-            nc.vector.tensor_copy(out=dst, in_=src)
-
-        def interleave_scalar(g, k):
-            m = split(g, k)
-            dst, src = views(g, k, m, P)
-            nc.scalar.copy(out=dst, in_=src)
-
-        def quantize_w(g, k):
+        def quantize_slab(g, k):
             w_codes[g, k] = keep.tile([P, SPAN], U32, name="w_codes%d_%d" % (g, k), align_bytes=64)
             w_plane[g, k] = keep.tile([P, SPAN], U8, name="w_plane%d_%d" % (g, k), align_bytes=64)
-            nc.vector.quantize_mx(out=w_codes[g, k][:].bitcast(FP8X4), scales=w_plane[g, k][:], in_=grouped[g, k][:])
-
-        acc = {}
+            nc.vector.quantize_mx(out=w_codes[g, k][:].bitcast(FP8X4), scales=w_plane[g, k][:], in_=mixed[g, k][:])
 
         def multiply(u, t, passes):
             g, s0, n = UNITS[u]
-            h, c0 = divmod(TIMES * s0, HALF)
+            h = s0 // HALF_STATIONS
             for k in passes:
                 if k == 0:
-                    acc[u, t] = psum.tile([P, TIMES * n], F32, name="acc%d" % t)
+                    product[g, h, t] = psum.tile([P, HALF], F32, name="product%d" % t)
                 nc.tensor.matmul_mx(
-                    out=acc[u, t][:],
+                    out=product[g, h, t][:],
                     lhsT=w_codes[g, k][:, P * t : P * (t + 1)].bitcast(FP8X4),
                     lhsT_scale=w_plane[g, k][:, P * t : P * (t + 1)],
-                    rhs=x_codes[h, k][:, c0 : c0 + TIMES * n].bitcast(FP8X4),
-                    rhs_scale=x_plane[:, k, TIMES * s0 : TIMES * (s0 + n)],
+                    rhs=x_codes[h, k][:].bitcast(FP8X4),
+                    rhs_scale=x_plane[:, k, HALF * h : HALF * (h + 1)],
                     start=(k == 0),
                     stop=(k == PASSES - 1),
                 )
 
         range_t = keep.tile([P, STATIONS], BF16)
         range_all = keep.tile([P, TOKENS], BF16)
-        params = keep.tile([P, PACK, PARAM_ROWS], F32)
+        constants = keep.tile([P, PACK, CONSTANT_ROWS], F32)
 
-        range_ps = psum.tile([P, TIMES], BF16, name="turn0")
+        range_ps = psum.tile([P, TIMES], BF16, name="turned0")
         nc.tensor.transpose(range_ps[:], range_rows[:], ident_bf[:])
         nc.vector.tensor_copy(out=range_t[:], in_=range_ps[:, 0:STATIONS])
-        param_ps = psum.tile([P, PACK, P], BF16, name="turn2")
+        constants_ps = psum.tile([P, PACK, P], BF16, name="turned2")
         for t in range(PACK):
-            nc.tensor.transpose(param_ps[:, t, :], param_rows[:, t:SPAN:PACK], ident_bf[:])
-        spread_ps = psum.tile([P, TOKENS], BF16, name="turn1")
+            nc.tensor.transpose(constants_ps[:, t, :], constant_rows[:, t:SPAN:PACK], ident_bf[:])
+        spread_ps = psum.tile([P, TOKENS], BF16, name="turned1")
         for s in range(STATIONS):
             nc.tensor.transpose(
                 spread_ps[:, TIMES * s : TIMES * (s + 1)], range_t[:, s : s + 1].to_broadcast([P, P]), ident_bf[:]
             )
-        interleave_vector(0, 0)
-        interleave_scalar(0, 0)
-        nc.vector.tensor_copy(out=params[:], in_=param_ps[:, :, 0:PARAM_ROWS])
-        quantize_w(0, 0)
+
+        interleave(0, 0, "vector")
+        interleave(0, 0, "scalar")
+        nc.vector.tensor_copy(out=constants[:], in_=constants_ps[:, :, 0:CONSTANT_ROWS])
+        quantize_slab(0, 0)
         for t in range(PACK):
             multiply(0, t, [0])
-        interleave_vector(0, 1)
-        interleave_scalar(0, 1)
-        nc.vector.tensor_copy(out=range_all[:], in_=spread_ps[:])
-        quantize_w(0, 1)
-        interleave_vector(0, 2)
-        interleave_scalar(0, 2)
-        for t in range(PACK):
+        interleave(0, 1, "vector")
+        interleave(0, 1, "scalar")
+        quantize_slab(0, 1)
+        interleave(0, 2, "vector")
+        interleave(0, 2, "scalar")
+        for t in range(PACK // 2):
             multiply(0, t, [1])
-        quantize_w(0, 2)
+        quantize_slab(0, 2)
+        nc.vector.tensor_copy(out=range_all[:], in_=spread_ps[:])
         for t in range(PACK):
-            multiply(0, t, [2])
-        interleave_scalar(1, 0)
+            multiply(0, t, [2] if t < PACK // 2 else [1, 2])
+        interleave(1, 0, "gpsimd")
 
         y = {}
         y_bf = {}
         turned = {}
-        y_plane = keep.tile([P, TOKENS], U8, align_bytes=64)
+        rows = {}
+        y_plane = keep.tile([P, GROUPS // 2, TOKENS], U8, align_bytes=64)
 
         def scale_and_offset(u, t):
             g, s0, n = UNITS[u]
+            h, c0 = divmod(TIMES * s0, HALF)
             if t == 0:
                 y[u] = work.tile([P, PACK, TIMES * n], F32, name="y")
             nc.vector.tensor_tensor(
-                out=y[u][:, t, :], in0=acc[u, t][:], in1=range_all[:, TIMES * s0 : TIMES * (s0 + n)], op=ALU.mult
+                out=y[u][:, t, :],
+                in0=product[g, h, t][:, c0 : c0 + TIMES * n],
+                in1=range_all[:, TIMES * s0 : TIMES * (s0 + n)],
+                op=ALU.mult,
             )
             for i in range(n):
                 row = (s0 + i) * GROUPS + g
                 part = y[u][:, t, TIMES * i : TIMES * (i + 1)]
-                nc.scalar.activation(out=part, in_=part, func=ACT.Identity, bias=params[:, t, row : row + 1])
+                nc.scalar.activation(out=part, in_=part, func=ACT.Identity, bias=constants[:, t, row : row + 1])
 
         def clip(u, t):
             g = UNITS[u][0]
             nc.vector.tensor_scalar(
                 out=y[u][:, t, :],
                 in0=y[u][:, t, :],
-                scalar1=params[:, t, LOW_ROW + g : LOW_ROW + g + 1],
-                scalar2=params[:, t, HIGH_ROW + g : HIGH_ROW + g + 1],
+                scalar1=constants[:, t, LOW_ROW + g : LOW_ROW + g + 1],
+                scalar2=constants[:, t, HIGH_ROW + g : HIGH_ROW + g + 1],
                 op0=ALU.max,
                 op1=ALU.min,
             )
 
         def round_y(u, n0, n1, engine):
             if n0 == 0:
-                y_bf[u] = work.tile([P, TIMES * UNITS[u][2] * PACK], BF16, name="y_bf", align_bytes=64, bufs=6)
+                y_bf[u] = work.tile([P, TIMES * UNITS[u][2] * PACK], BF16, name="y_bf", align_bytes=64)
             dst = y_bf[u][:].rearrange("p (n i t) -> p n t i", i=2, t=PACK)[:, n0 // 2 : n1 // 2]
             src = y[u][:].rearrange("p t (n i) -> p n t i", i=2)[:, n0 // 2 : n1 // 2]
             if engine == "gpsimd":
-                nc.gpsimd.tensor_scalar(out=dst, in0=src, scalar1=1.0, scalar2=1.0, op0=ALU.mult, op1=ALU.mult)
+                copy_on_gpsimd(dst, src)
             elif engine == "scalar":
                 nc.scalar.copy(out=dst, in_=src)
             else:
@@ -222,99 +231,105 @@ def tile_calibrated_clipped_channels_g6_kernel(
             y_codes = work.tile([P, TIMES * n], U32, name="y_codes", align_bytes=64)
             nc.vector.quantize_mx(
                 out=y_codes[:].bitcast(FP8X4),
-                scales=y_plane[4 * g : P, TIMES * s0 : TIMES * (s0 + n)],
+                scales=y_plane[4 * (g % 2) : P, g // 2, TIMES * s0 : TIMES * (s0 + n)],
                 in_=y_bf[u][:],
             )
-            dst = out_1[g].rearrange("p n t -> p (n t)")[:, PACK * TIMES * s0 : PACK * TIMES * (s0 + n)]
-            nc.sync.dma_start(out=dst.bitcast(I32), in_=y_codes[:].bitcast(I32))
+            part = out_1[g].rearrange("p n t -> p (n t)")[:, PACK * TIMES * s0 : PACK * TIMES * (s0 + n)]
+            nc.sync.dma_start(out=part.bitcast(I32), in_=y_codes[:].bitcast(I32))
 
-        def store_scales(n0, n1):
-            for q in range(4):
+        def store_scales(pair):
+            for q in range(QUADRANTS):
                 nc.sync.dma_start(
-                    out=out_2[:, 4 * q : 4 * q + 4, n0:n1].bitcast(I32),
-                    in_=y_plane[32 * q : 32 * q + 4 * GROUPS, n0:n1].bitcast(I32),
+                    out=out_2[2 * pair : 2 * pair + 2, 4 * q : 4 * q + 4, :].bitcast(I32),
+                    in_=y_plane[32 * q : 32 * q + 8, pair, :].bitcast(I32),
                 )
 
         def turn(u, i, t):
             s0 = UNITS[u][1]
             if t == 0:
-                turned[u, i] = psum.tile([P, PACK, P], F32, name="turn%d" % ((s0 + i) % 4))
+                turned[u, i] = psum.tile([P, PACK, P], F32, name="turned%d" % ((s0 + i) % HALF_STATIONS))
             nc.tensor.transpose(turned[u, i][:, t, :], y[u][:, t, TIMES * i : TIMES * (i + 1)], ident[:])
 
-        def store_y(u, i, on_vector):
+        def store_y(u, i, engine):
             g, s0, n = UNITS[u]
-            rows = work.tile([P, SPAN], F32, name="rows", bufs=8)
-            dst = rows[:].rearrange("p (m t) -> p m t", t=PACK)
+            width = 1 if u == LAST else 2
+            first = i - i % width
+            if i == first:
+                rows[u, first] = work.tile([P, width, SPAN], F32, name="rows", bufs=6)
+            dst = rows[u, first][:, i - first, :].rearrange("p (m t) -> p m t", t=PACK)
             src = turned[u, i][:].rearrange("p t m -> p m t")
-            if on_vector:
+            if engine == "vector":
                 nc.vector.tensor_copy(out=dst, in_=src)
             else:
                 nc.scalar.copy(out=dst, in_=src)
-            nc.sync.dma_start(out=out_0[s0 + i, :, SPAN * g : SPAN * (g + 1)], in_=rows[:])
+            if i == first + width - 1:
+                part = out_0[s0 + first : s0 + first + width, :, SPAN * g : SPAN * (g + 1)]
+                nc.sync.dma_start(out=part.rearrange("s p c -> p s c"), in_=rows[u, first][:])
 
-        last = len(UNITS) - 1
-        for u in range(last + 1):
-            g, s0, n = UNITS[u]
+        for u, (g, s0, n) in enumerate(UNITS):
             before = UNITS[u - 1][2] if u > 0 else 0
-            full = n == HALF_STATIONS
-            shared = min(GPSIMD_TOKENS if full else 224, TIMES * before) if before >= GPSIMD_STATIONS else 0
-            on_vector = VECTOR_STORES if full else 1
-            new_group = u < last and UNITS[u + 1][0] != g
-            early = g + 1 < GROUPS and not new_group
-            if shared:
+            prepares = g + 1 < GROUPS
+            opens = prepares and s0 == 0
+            closes = prepares and s0 > 0
+            vector_banks = 1 if prepares and u > 0 else 0
+            shared = min(GPSIMD_TOKENS_PER_STATION * n + GPSIMD_TOKENS_PER_BANK * vector_banks, TIMES * before)
+
+            if u > 0:
                 round_y(u - 1, 0, shared, "gpsimd")
             for t in range(PACK):
-                if t < before:
-                    for tt in range(PACK):
-                        turn(u - 1, t, tt)
+                if t % 2 == 0:
+                    for i in range(t, min(t + 2, before)):
+                        for tt in range(PACK):
+                            turn(u - 1, i, tt)
                 scale_and_offset(u, t)
-                if u < last:
-                    multiply(u + 1, t, [0] if new_group else [0, 1, 2])
-            for i in range(min(before, on_vector)):
-                store_y(u - 1, i, True)
-            if shared < TIMES * before:
+                if u < LAST and UNITS[u + 1][1] % HALF_STATIONS == 0:
+                    multiply(u + 1, t, [0] if closes else range(PASSES))
+            for i in range(vector_banks):
+                store_y(u - 1, i, "vector")
+
+            if u > 0:
                 round_y(u - 1, shared, TIMES * before, "vector")
-            if early:
-                interleave_vector(g + 1, 0)
-                interleave_vector(g + 1, 1)
-            elif new_group:
-                interleave_vector(g + 1, 2)
-                quantize_w(g + 1, 1)
+            if opens:
+                interleave(g + 1, 0, "vector")
+                interleave(g + 1, 1, "vector")
+            elif closes:
+                interleave(g + 1, 2, "vector")
+                quantize_slab(g + 1, 1)
                 for t in range(PACK):
                     multiply(u + 1, t, [1])
-            else:
-                clip(u, 0)
-            if u == last:
+            clip(u, 0)
+            if u == LAST:
                 quantize_y(u - 1)
-            for i in range(on_vector, before):
-                store_y(u - 1, i, False)
-            if early:
-                interleave_scalar(g + 1, 1)
-                interleave_scalar(g + 1, 2)
-            elif new_group and g + 2 < GROUPS:
-                interleave_scalar(g + 2, 0)
+            for i in range(vector_banks, before):
+                store_y(u - 1, i, "scalar")
+            if opens:
+                interleave(g + 1, 1, "scalar")
+                interleave(g + 1, 2, "scalar")
+            elif closes and g + 2 < GROUPS:
+                interleave(g + 2, 0, "scalar")
+            if opens and u > 0:
+                quantize_slab(g + 1, 0)
+            elif closes:
+                quantize_slab(g + 1, 2)
+                for t in range(PACK):
+                    multiply(u + 1, t, [2])
             for t in range(PACK):
-                if t == 1 and early and u > 0:
-                    quantize_w(g + 1, 0)
-                if t == 1 and new_group:
-                    quantize_w(g + 1, 2)
-                    for tt in range(PACK):
-                        multiply(u + 1, tt, [2])
-                if early or new_group or t > 0:
+                if t > 0:
                     clip(u, t)
-                if u == last:
+                if u == LAST:
                     for i in range(n):
                         turn(u, i, t)
             if u == 0:
-                quantize_w(1, 0)
-            elif u < last:
+                quantize_slab(1, 0)
+            elif u < LAST:
                 quantize_y(u - 1)
-            if u == last - 1:
-                store_scales(0, HALF)
+            if (g, s0) == (GROUPS // 2, 0):
+                store_scales(0)
 
-        round_y(last, 0, TIMES * UNITS[last][2] - 64, "vector")
-        round_y(last, TIMES * UNITS[last][2] - 64, TIMES * UNITS[last][2], "scalar")
-        store_y(last, 0, False)
-        quantize_y(last)
-        store_y(last, 1, False)
-        store_scales(HALF, TOKENS)
+        tokens = TIMES * UNITS[LAST][2]
+        round_y(LAST, 0, tokens - SCALAR_LAST_TOKENS, "vector")
+        round_y(LAST, tokens - SCALAR_LAST_TOKENS, tokens, "scalar")
+        store_y(LAST, 0, "scalar")
+        store_y(LAST, 1, "vector")
+        quantize_y(LAST)
+        store_scales(1)

from contextlib import ExitStack

import concourse.mybir as mybir
from concourse.masks import make_identity

F32 = mybir.dt.float32
BF16 = mybir.dt.bfloat16
I32 = mybir.dt.int32
U32 = mybir.dt.uint32
U8 = mybir.dt.uint8
FP8X4 = mybir.dt.float8_e4m3fn_x4
ALU = mybir.AluOpType
ACT = mybir.ActivationFunctionType

STATIONS, TIMES, SENSORS, CHANNELS = 8, 128, 1536, 2048
TOKENS = STATIONS * TIMES
FLOPS = 2 * TOKENS * SENSORS * CHANNELS

P = 128
PACK = 4
QUADRANTS = 4
SPAN = P * PACK
PASSES = SENSORS // SPAN
GROUPS = CHANNELS // SPAN
HALF = TOKENS // 2
HALF_STATIONS = STATIONS // 2

UNITS = [(g, s, HALF_STATIONS) for g in range(GROUPS) for s in (0, HALF_STATIONS)][:-1]
UNITS = UNITS + [(GROUPS - 1, s, 2) for s in (HALF_STATIONS, HALF_STATIONS + 2)]
LAST = len(UNITS) - 1

VECTOR_COLUMNS_FIRST = 64
VECTOR_COLUMNS = (24, 48, 48)
GPSIMD_TOKENS_PER_STATION = 80
GPSIMD_TOKENS_PER_BANK = 96
SCALAR_LAST_TOKENS = 96

LOW_ROW = STATIONS * GROUPS
HIGH_ROW = LOW_ROW + GROUPS
CONSTANT_ROWS = HIGH_ROW + GROUPS


def tile_calibrated_clipped_channels_g6_kernel(
    tc, x_words, x_scales, calibration, range_factor, offset, low, high, out_0, out_1, out_2
):
    nc = tc.nc
    with ExitStack() as ctx:
        keep = ctx.enter_context(tc.tile_pool(name="keep", bufs=1))
        work = ctx.enter_context(tc.tile_pool(name="work", bufs=3))
        psum = ctx.enter_context(tc.psum_pool(name="psum", bufs=1))
        ctx.enter_context(tc.manual_schedule())

        range_rows = keep.tile([P, TIMES], BF16)
        x_plane = keep.tile([P, PASSES, TOKENS], U8, align_bytes=64)
        constant_rows = keep.tile([P, SPAN], BF16)
        nc.vector.memset(range_rows[:], 0.0)
        nc.vector.memset(constant_rows[:], 0.0)
        nc.vector.memset(x_plane[:].rearrange("p k n -> p (k n)").bitcast(I32), 0)
        ident = keep.tile([P, P], F32)
        make_identity(nc, ident[:])

        nc.scalar.dma_start(out=range_rows[0:STATIONS, :], in_=range_factor)
        nc.scalar.dma_start(out=constant_rows[0:LOW_ROW, :], in_=offset.rearrange("s (g c) -> (s g) c", g=GROUPS))
        nc.scalar.dma_start(out=constant_rows[LOW_ROW:HIGH_ROW, :], in_=low.rearrange("(g c) -> g c", g=GROUPS))
        nc.scalar.dma_start(out=constant_rows[HIGH_ROW:CONSTANT_ROWS, :], in_=high.rearrange("(g c) -> g c", g=GROUPS))
        ident_bf = keep.tile([P, P], BF16)
        nc.scalar.activation(out=ident_bf[:], in_=ident[:], func=ACT.Identity)

        slab = {}
        x_codes = {}

        def load_slab(g, k):
            slab[g, k] = keep.tile([P, PACK, SPAN], BF16, name="slab%d_%d" % (g, k))
            part = calibration[SPAN * k : SPAN * (k + 1), SPAN * g : SPAN * (g + 1)]
            nc.sync.dma_start(out=slab[g, k][:], in_=part.rearrange("(p j) c -> p j c", j=PACK))

        def load_x(h, k):
            x_codes[h, k] = keep.tile([P, HALF], U32, name="x_codes%d_%d" % (h, k), align_bytes=64)
            part = x_words[k].rearrange("p n j -> p (n j)")[:, PACK * HALF * h : PACK * HALF * (h + 1)]
            nc.sync.dma_start(out=x_codes[h, k][:].bitcast(I32), in_=part.bitcast(I32))

        load_slab(0, 0)
        load_x(0, 0)
        load_slab(0, 1)
        load_slab(0, 2)
        for q in range(QUADRANTS):
            nc.sync.dma_start(
                out=x_plane[32 * q : 32 * q + 4, :, :].bitcast(I32),
                in_=x_scales[:, 4 * q : 4 * q + 4, :].rearrange("k r n -> r k n").bitcast(I32),
            )
        load_x(0, 1)
        load_x(0, 2)
        load_slab(1, 0)
        for k in range(PASSES):
            load_x(1, k)
        for g in range(1, GROUPS):
            for k in range(PASSES):
                if (g, k) not in slab:
                    load_slab(g, k)

        mixed = {}
        w_codes = {}
        w_plane = {}
        product = {}

        def interleave(g, k, engine):
            if (g, k) not in mixed:
                if (g, k) in ((0, PASSES - 1), (1, 0)):
                    mixed[g, k] = keep.tile([P, PACK * SPAN], BF16, name="mixed_shared", align_bytes=64)
                else:
                    mixed[g, k] = work.tile([P, PACK * SPAN], BF16, name="mixed", align_bytes=64, bufs=4)
            split = VECTOR_COLUMNS_FIRST if g == 0 else VECTOR_COLUMNS[k]
            if engine == "gpsimd":
                dst = mixed[g, k][:].rearrange("p (t m j) -> p m t j", t=PACK, j=PACK)[:, split:P]
                src = slab[g, k][:].rearrange("p j (m t) -> p m t j", t=PACK)[:, split:P]
                copy_on_gpsimd(dst, src)
                return
            dst = mixed[g, k][:].rearrange("p (t m i j) -> p m t j i", t=PACK, i=2, j=PACK)
            src = slab[g, k][:].rearrange("p j (m i t) -> p m t j i", i=2, t=PACK)
            if engine == "vector":
                nc.vector.tensor_copy(out=dst[:, 0 : split // 2], in_=src[:, 0 : split // 2])
            else:
                nc.scalar.copy(out=dst[:, split // 2 : P // 2], in_=src[:, split // 2 : P // 2])

        def copy_on_gpsimd(dst, src):
            nc.gpsimd.tensor_scalar(out=dst, in0=src, scalar1=1.0, scalar2=1.0, op0=ALU.mult, op1=ALU.mult)

        def quantize_slab(g, k):
            w_codes[g, k] = keep.tile([P, SPAN], U32, name="w_codes%d_%d" % (g, k), align_bytes=64)
            w_plane[g, k] = keep.tile([P, SPAN], U8, name="w_plane%d_%d" % (g, k), align_bytes=64)
            nc.vector.quantize_mx(out=w_codes[g, k][:].bitcast(FP8X4), scales=w_plane[g, k][:], in_=mixed[g, k][:])

        def multiply(u, t, passes):
            g, s0, n = UNITS[u]
            h = s0 // HALF_STATIONS
            for k in passes:
                if k == 0:
                    product[g, h, t] = psum.tile([P, HALF], F32, name="product%d" % t)
                nc.tensor.matmul_mx(
                    out=product[g, h, t][:],
                    lhsT=w_codes[g, k][:, P * t : P * (t + 1)].bitcast(FP8X4),
                    lhsT_scale=w_plane[g, k][:, P * t : P * (t + 1)],
                    rhs=x_codes[h, k][:].bitcast(FP8X4),
                    rhs_scale=x_plane[:, k, HALF * h : HALF * (h + 1)],
                    start=(k == 0),
                    stop=(k == PASSES - 1),
                )

        range_t = keep.tile([P, STATIONS], BF16)
        range_all = keep.tile([P, TOKENS], BF16)
        constants = keep.tile([P, PACK, CONSTANT_ROWS], F32)

        range_ps = psum.tile([P, TIMES], BF16, name="turned0")
        nc.tensor.transpose(range_ps[:], range_rows[:], ident_bf[:])
        nc.vector.tensor_copy(out=range_t[:], in_=range_ps[:, 0:STATIONS])
        constants_ps = psum.tile([P, PACK, P], BF16, name="turned2")
        for t in range(PACK):
            nc.tensor.transpose(constants_ps[:, t, :], constant_rows[:, t:SPAN:PACK], ident_bf[:])
        spread_ps = psum.tile([P, TOKENS], BF16, name="turned1")
        for s in range(STATIONS):
            nc.tensor.transpose(
                spread_ps[:, TIMES * s : TIMES * (s + 1)], range_t[:, s : s + 1].to_broadcast([P, P]), ident_bf[:]
            )

        interleave(0, 0, "vector")
        interleave(0, 0, "scalar")
        nc.vector.tensor_copy(out=constants[:], in_=constants_ps[:, :, 0:CONSTANT_ROWS])
        quantize_slab(0, 0)
        for t in range(PACK):
            multiply(0, t, [0])
        interleave(0, 1, "vector")
        interleave(0, 1, "scalar")
        quantize_slab(0, 1)
        interleave(0, 2, "vector")
        interleave(0, 2, "scalar")
        for t in range(PACK // 2):
            multiply(0, t, [1])
        quantize_slab(0, 2)
        nc.vector.tensor_copy(out=range_all[:], in_=spread_ps[:])
        for t in range(PACK):
            multiply(0, t, [2] if t < PACK // 2 else [1, 2])
        interleave(1, 0, "gpsimd")

        y = {}
        y_bf = {}
        turned = {}
        rows = {}
        y_plane = keep.tile([P, GROUPS // 2, TOKENS], U8, align_bytes=64)

        def scale_and_offset(u, t):
            g, s0, n = UNITS[u]
            h, c0 = divmod(TIMES * s0, HALF)
            if t == 0:
                y[u] = work.tile([P, PACK, TIMES * n], F32, name="y")
            nc.vector.tensor_tensor(
                out=y[u][:, t, :],
                in0=product[g, h, t][:, c0 : c0 + TIMES * n],
                in1=range_all[:, TIMES * s0 : TIMES * (s0 + n)],
                op=ALU.mult,
            )
            for i in range(n):
                row = (s0 + i) * GROUPS + g
                part = y[u][:, t, TIMES * i : TIMES * (i + 1)]
                nc.scalar.activation(out=part, in_=part, func=ACT.Identity, bias=constants[:, t, row : row + 1])

        def clip(u, t):
            g = UNITS[u][0]
            nc.vector.tensor_scalar(
                out=y[u][:, t, :],
                in0=y[u][:, t, :],
                scalar1=constants[:, t, LOW_ROW + g : LOW_ROW + g + 1],
                scalar2=constants[:, t, HIGH_ROW + g : HIGH_ROW + g + 1],
                op0=ALU.max,
                op1=ALU.min,
            )

        def round_y(u, n0, n1, engine):
            if n0 == 0:
                y_bf[u] = work.tile([P, TIMES * UNITS[u][2] * PACK], BF16, name="y_bf", align_bytes=64)
            dst = y_bf[u][:].rearrange("p (n i t) -> p n t i", i=2, t=PACK)[:, n0 // 2 : n1 // 2]
            src = y[u][:].rearrange("p t (n i) -> p n t i", i=2)[:, n0 // 2 : n1 // 2]
            if engine == "gpsimd":
                copy_on_gpsimd(dst, src)
            elif engine == "scalar":
                nc.scalar.copy(out=dst, in_=src)
            else:
                nc.vector.tensor_copy(out=dst, in_=src)

        def quantize_y(u):
            g, s0, n = UNITS[u]
            y_codes = work.tile([P, TIMES * n], U32, name="y_codes", align_bytes=64)
            nc.vector.quantize_mx(
                out=y_codes[:].bitcast(FP8X4),
                scales=y_plane[4 * (g % 2) : P, g // 2, TIMES * s0 : TIMES * (s0 + n)],
                in_=y_bf[u][:],
            )
            part = out_1[g].rearrange("p n t -> p (n t)")[:, PACK * TIMES * s0 : PACK * TIMES * (s0 + n)]
            nc.sync.dma_start(out=part.bitcast(I32), in_=y_codes[:].bitcast(I32))

        def store_scales(pair):
            for q in range(QUADRANTS):
                nc.sync.dma_start(
                    out=out_2[2 * pair : 2 * pair + 2, 4 * q : 4 * q + 4, :].bitcast(I32),
                    in_=y_plane[32 * q : 32 * q + 8, pair, :].bitcast(I32),
                )

        def turn(u, i, t):
            s0 = UNITS[u][1]
            if t == 0:
                turned[u, i] = psum.tile([P, PACK, P], F32, name="turned%d" % ((s0 + i) % HALF_STATIONS))
            nc.tensor.transpose(turned[u, i][:, t, :], y[u][:, t, TIMES * i : TIMES * (i + 1)], ident[:])

        def store_y(u, i, engine):
            g, s0, n = UNITS[u]
            width = 1 if u == LAST else 2
            first = i - i % width
            if i == first:
                rows[u, first] = work.tile([P, width, SPAN], F32, name="rows", bufs=6)
            dst = rows[u, first][:, i - first, :].rearrange("p (m t) -> p m t", t=PACK)
            src = turned[u, i][:].rearrange("p t m -> p m t")
            if engine == "vector":
                nc.vector.tensor_copy(out=dst, in_=src)
            else:
                nc.scalar.copy(out=dst, in_=src)
            if i == first + width - 1:
                part = out_0[s0 + first : s0 + first + width, :, SPAN * g : SPAN * (g + 1)]
                nc.sync.dma_start(out=part.rearrange("s p c -> p s c"), in_=rows[u, first][:])

        for u, (g, s0, n) in enumerate(UNITS):
            before = UNITS[u - 1][2] if u > 0 else 0
            prepares = g + 1 < GROUPS
            opens = prepares and s0 == 0
            closes = prepares and s0 > 0
            vector_banks = 1 if prepares and u > 0 else 0
            shared = min(GPSIMD_TOKENS_PER_STATION * n + GPSIMD_TOKENS_PER_BANK * vector_banks, TIMES * before)

            if u > 0:
                round_y(u - 1, 0, shared, "gpsimd")
            for t in range(PACK):
                if t % 2 == 0:
                    for i in range(t, min(t + 2, before)):
                        for tt in range(PACK):
                            turn(u - 1, i, tt)
                scale_and_offset(u, t)
                if u < LAST and UNITS[u + 1][1] % HALF_STATIONS == 0:
                    multiply(u + 1, t, [0] if closes else range(PASSES))
            for i in range(vector_banks):
                store_y(u - 1, i, "vector")

            if u > 0:
                round_y(u - 1, shared, TIMES * before, "vector")
            if opens:
                interleave(g + 1, 0, "vector")
                interleave(g + 1, 1, "vector")
            elif closes:
                interleave(g + 1, 2, "vector")
                quantize_slab(g + 1, 1)
                for t in range(PACK):
                    multiply(u + 1, t, [1])
            clip(u, 0)
            if u == LAST:
                quantize_y(u - 1)
            for i in range(vector_banks, before):
                store_y(u - 1, i, "scalar")
            if opens:
                interleave(g + 1, 1, "scalar")
                interleave(g + 1, 2, "scalar")
            elif closes and g + 2 < GROUPS:
                interleave(g + 2, 0, "scalar")
            if opens and u > 0:
                quantize_slab(g + 1, 0)
            elif closes:
                quantize_slab(g + 1, 2)
                for t in range(PACK):
                    multiply(u + 1, t, [2])
            for t in range(PACK):
                if t > 0:
                    clip(u, t)
                if u == LAST:
                    for i in range(n):
                        turn(u, i, t)
            if u == 0:
                quantize_slab(1, 0)
            elif u < LAST:
                quantize_y(u - 1)
            if (g, s0) == (GROUPS // 2, 0):
                store_scales(0)

        tokens = TIMES * UNITS[LAST][2]
        round_y(LAST, 0, tokens - SCALAR_LAST_TOKENS, "vector")
        round_y(LAST, tokens - SCALAR_LAST_TOKENS, tokens, "scalar")
        store_y(LAST, 0, "scalar")
        store_y(LAST, 1, "vector")
        quantize_y(LAST)
        store_scales(1)
